import numpy as np
import ml_dtypes


def mxq(x, axis, fmt="e4m3"):
    dtype, down = {"e4m3": (ml_dtypes.float8_e4m3fn, 7), "e5m2": (ml_dtypes.float8_e5m2, 14)}[fmt]
    v = np.moveaxis(np.asarray(x, np.float32).astype(ml_dtypes.bfloat16).astype(np.float64), axis, -1)
    blocks = v.reshape(v.shape[:-1] + (-1, 32))
    amax = np.abs(blocks).max(-1, keepdims=True)
    byte = np.maximum(np.where(amax > 0, np.frexp(amax)[1] - 1 + 127, 0) - down, 1)
    scale = np.exp2(byte - 127.0)
    codes = (blocks / scale).astype(np.float32).astype(dtype).astype(np.float64)
    return np.moveaxis((codes * scale).reshape(v.shape), -1, axis)


WIDE = False


def mx_kscale(k):
    if not WIDE:
        return np.ones(k)
    levels = np.array([10, -10, 5, -5, 0])
    if k % 512:
        return np.exp2(np.random.permutation(np.resize(levels, k // 32))).repeat(32)
    a = np.empty((k // 512, 16))
    for p in range(k // 512):
        a[p, :8] = np.random.permutation(np.resize(levels, 8))
        for g in range(8):
            far = levels[np.abs(levels - a[p, g]) >= 10]
            a[p, g + 8] = far[np.random.randint(len(far))]
    return np.exp2(a.ravel()).repeat(32)


def f64(x):
    return np.asarray(x).astype(np.float64)


def striped(idx):
    return np.tile(idx.reshape(-1, 16).T, (8, 1)).astype(np.uint16)


def unstriped(offs):
    return offs[:16].T.reshape(-1).astype(np.int64)


def striped8(idx):
    return np.concatenate([x.reshape(-1, 16).T for x in idx]).astype(np.uint16)


def runs(offs, k):
    lists = np.stack([offs[16 * r : 16 * r + 16].T.reshape(-1) for r in range(8)]).astype(np.int64)
    return lists[np.arange(k) % 512 // 64]


def pack_weight(w):
    k, n = w.shape
    w = f64(np.asarray(w, np.float32).astype(ml_dtypes.bfloat16)).reshape(k // 32, 32, n)
    amax = np.abs(w).max(1)
    byte = np.clip(np.where(amax > 0, np.frexp(amax)[1] - 1 + 127 - 7, 1), 1, 254)
    scaled = (w * np.exp2(127.0 - byte)[:, None, :]).reshape(k, n).astype(np.float32)
    words = np.ascontiguousarray(scaled.reshape(k // 512, 128, 4, n).transpose(0, 1, 3, 2)).astype(ml_dtypes.float8_e4m3fn).view(np.uint8)
    return words, np.ascontiguousarray(byte.astype(np.uint8).reshape(k // 512, 16, n))


def unpack_weight(words, scales):
    g, p, n, _ = words.shape
    vals = np.ascontiguousarray(words).view(ml_dtypes.float8_e4m3fn).astype(np.float64) * np.repeat(np.exp2(scales.astype(np.float64) - 127.0), 8, axis=1)[..., None]
    return vals.transpose(0, 1, 3, 2).reshape(g * 512, n)


K, T, S, G, H = 512, 2048, 512, 2048, 512


def setup_inputs():
    n = np.random.standard_normal
    s = mx_kscale(K)[:, None]
    packed_xT = pack_weight(n((K, T)) * s)
    packed_dT = pack_weight(n((K, G)) / s)
    return {
        "x_words": packed_xT[0],
        "x_scales": packed_xT[1],
        "d_words": packed_dT[0],
        "d_scales": packed_dT[1],
        "gs": (np.random.uniform(0.5, 1.5, (K, 1)) * s).astype(np.float32),
        "offs": striped(np.random.permutation(T)[:S]),
        "k1": striped8(np.random.randint(0, G, (8, H))),
        "nb": striped8(np.stack([np.random.permutation(S) for _ in range(8)])),
    }


def reference(x_words, x_scales, d_words, d_scales, gs, offs, k1, nb):
    d_k1 = unpack_weight(d_words, d_scales)[np.arange(K)[:, None], runs(k1, K)]
    xq = unpack_weight(x_words, x_scales)[:, unstriped(offs)]
    h = np.tanh(0.0625 * (d_k1.T @ xq))
    z = f64(gs) * (h[np.arange(H)[:, None], runs(nb, H)])
    h2 = 0.0625 * ((d_k1.T @ mxq(z, 0, "e4m3")))
    return h2

@@ -1,0 +1,161 @@
+from contextlib import ExitStack
+
+import concourse.mybir as mybir
+
+F32 = mybir.dt.float32
+BF16 = mybir.dt.bfloat16
+I32 = mybir.dt.int32
+U32 = mybir.dt.uint32
+U16 = mybir.dt.uint16
+U8 = mybir.dt.uint8
+FP8X4 = mybir.dt.float8_e4m3fn_x4
+TANH = mybir.ActivationFunctionType.Tanh
+COPY = mybir.ActivationFunctionType.Copy
+MULT = mybir.AluOpType.mult
+
+P = 128
+PACK = 4
+S = 512
+TABLE = 2048
+HALF = 256
+CHUNK = 128
+FLOPS = 2 * 2 * 512 * 512 * 512
+
+
+def tile_picked_pqtwice_tanh_p_kernel(
+    tc, x_words, x_scales, d_words, d_scales, gs, offs, k1, nb, out
+):
+    nc = tc.nc
+    with ExitStack() as ctx:
+        keep = ctx.enter_context(tc.tile_pool(name="keep", bufs=1))
+        psum = ctx.enter_context(tc.psum_pool(name="psum", bufs=1))
+
+        k1_t = keep.tile([P, S // 16], U16, name="k1_t")
+        offs_t = keep.tile([P, S // 16], U16, name="offs_t")
+        nb_t = keep.tile([P, S // 16], U16, name="nb_t")
+        dsc_win = keep.tile([P, TABLE], U8, name="dsc_win", align_bytes=64)
+        xsc_win = keep.tile([P, TABLE], U8, name="xsc_win", align_bytes=64)
+        dw_win = keep.tile([P, TABLE], U32, name="dw_win", align_bytes=64)
+        xw_win = keep.tile([P, TABLE], U32, name="xw_win", align_bytes=64)
+        gs_t = keep.tile([P, PACK], F32, name="gs_t")
+        warm = keep.tile([P, 2], F32, name="warm")
+
+        nc.vector.memset(xsc_win[:].bitcast(I32), 0)
+        nc.vector.memset(warm[:, 0:1], 0.0)
+        nc.sync.dma_start(k1_t[:], k1)
+        nc.sync.dma_start(
+            out=dsc_win[:].bitcast(I32),
+            in_=d_scales.rearrange("z q c -> q z c").bitcast(I32).to_broadcast([16, 8, TABLE // 4]),
+        )
+        nc.sync.dma_start(out=dw_win[:].bitcast(I32), in_=d_words[0].rearrange("p n t -> p (n t)").bitcast(I32))
+        nc.sync.dma_start(offs_t[:], offs)
+        nc.sync.dma_start(nb_t[:], nb)
+        for q in range(4):
+            nc.scalar.dma_start(
+                out=xsc_win[32 * q : 32 * q + 4, :].bitcast(I32), in_=x_scales[0, 4 * q : 4 * q + 4, :].bitcast(I32)
+            )
+        nc.sync.dma_start(out=xw_win[:].bitcast(I32), in_=x_words[0].rearrange("p n t -> p (n t)").bitcast(I32))
+        nc.gpsimd.dma_start(out=gs_t[:], in_=gs.rearrange("(p t) o -> p (t o)", t=PACK))
+        nc.scalar.activation(warm[:, 1:2], warm[:, 0:1], TANH)
+
+        dsc_g = keep.tile([P, S], U8, name="dsc_g", align_bytes=64)
+        dsc = keep.tile([P, S], U8, name="dsc", align_bytes=64)
+        nc.vector.tensor_copy(dsc_g[:], dsc_win[:].indirect(k1_t[:]))
+        nc.vector.tensor_copy(
+            dsc[:].rearrange("p (t m) -> p m t", t=PACK), dsc_g[:].rearrange("p (m t) -> p m t", t=PACK)
+        )
+        for j in range(1, 4):
+            nc.sync.dma_start(out=dsc[j:P:32, :].bitcast(I32), in_=dsc[8 * j : P : 32, :].bitcast(I32))
+
+        dw_g = keep.tile([P, S], U32, name="dw_g", align_bytes=64)
+        dw = keep.tile([P, S], U32, name="dw", align_bytes=64)
+        dealt = dw[:].rearrange("p (t m) -> p m t", t=PACK)
+        picked = dw_g[:].rearrange("p (m t) -> p m t", t=PACK)
+        nc.vector.tensor_copy(dw_g[:], dw_win[:].indirect(k1_t[:]))
+        xsc = keep.tile([P, S], U8, name="xsc", align_bytes=64)
+        nc.vector.tensor_copy(xsc[:], xsc_win[:].indirect(offs_t[:]))
+        nc.vector.tensor_copy(dealt[:, :, 0:1], picked[:, :, 0:1])
+
+        xw = keep.tile([P, S], U32, name="xw", align_bytes=64)
+        for c in range(2):
+            nc.vector.tensor_copy(xw[:, c * HALF : (c + 1) * HALF], xw_win[:].indirect(offs_t[:, 16 * c : 16 * (c + 1)]))
+        nc.vector.tensor_copy(dealt[:, :, 1:PACK], picked[:, :, 1:PACK])
+
+        zg = keep.tile([P, PACK * S + CHUNK], BF16, name="zg", align_bytes=64)
+        h = [keep.tile([P, S], F32, name=f"h{t}", align_bytes=64)[:] for t in range(PACK - 1)]
+        h.append(zg[:, 2 * S + CHUNK :].bitcast(F32))
+        hz = [keep.tile([P, S], F32, name=f"hz{t}", align_bytes=64) for t in range(PACK)]
+
+        def product(acc, t, words, scales):
+            cols = slice(P * t, P * (t + 1))
+            nc.tensor.matmul_mx(
+                out=acc,
+                lhsT=dw[:, cols].bitcast(FP8X4),
+                lhsT_scale=dsc[:, cols],
+                rhs=words.bitcast(FP8X4),
+                rhs_scale=scales,
+                start=True,
+                stop=True,
+            )
+
+        def first(t, part, bank):
+            acc = psum.tile([P, part.stop - part.start], F32, name="acc", tag=f"bank{bank}")
+            product(acc[:], t, xw[:, part], xsc[:, part])
+            nc.scalar.activation(h[t][:, part], acc[:], TANH, scale=0.0625)
+
+        def weigh(t):
+            nc.scalar.activation(hz[t][:], h[t], COPY, scale=gs_t[:, t : t + 1])
+
+        def fetch(t, c0, width):
+            lst = nb_t[:, c0 // 16 : (c0 + width) // 16]
+            nc.vector.tensor_copy(zg[:, S * t + c0 : S * t + c0 + width], hz[t][:].indirect(lst))
+
+        for c in range(2):
+            part = slice(c * HALF, (c + 1) * HALF)
+            first(0, part, c)
+            nc.vector.tensor_scalar(hz[0][:, part], h[0][:, part], gs_t[:, 0:1], None, MULT)
+        whole = slice(0, S)
+        first(1, whole, 2)
+        first(2, whole, 3)
+        weigh(1)
+        first(3, whole, 4)
+        weigh(2)
+        weigh(3)
+
+        for t in range(2):
+            for c0 in range(0, S, HALF):
+                fetch(t, c0, HALF)
+
+        chunks = S // CHUNK
+        planes = zg[:, 0 : PACK * S].rearrange("p (t n) -> p t n", t=PACK)
+        zi = [keep.tile([P, CHUNK, PACK], BF16, name=f"zi{c}", align_bytes=64) for c in range(chunks)]
+        for c in range(chunks):
+            fetch(2, c * CHUNK, CHUNK)
+            fetch(3, c * CHUNK, CHUNK)
+            dst = zi[c][:].rearrange("p (n i) t -> p n t i", i=4)
+            src = planes[:, :, c * CHUNK : (c + 1) * CHUNK].rearrange("p t (n i) -> p n t i", i=4)
+            if c < chunks - 1:
+                nc.scalar.copy(dst, src)
+            else:
+                nc.vector.tensor_copy(dst, src)
+
+        out_v = out.rearrange("(p t) n -> p t n", t=PACK)
+        bank = 5
+        for c in range(chunks):
+            zq = keep.tile([P, CHUNK], U32, name=f"zq{c}", align_bytes=64)
+            zs = keep.tile([P, CHUNK], U8, name=f"zs{c}", align_bytes=64)
+            nc.vector.quantize_mx(out=zq[:].bitcast(FP8X4), scales=zs[:], in_=zi[c][:].rearrange("p n t -> p (n t)"))
+            group = PACK if c < chunks - 1 else 2
+            for u in range(PACK // group):
+                acc2 = psum.tile([P, group, CHUNK], F32, name="acc2", tag=f"bank{bank % 8}")
+                bank += 1
+                for v in range(group):
+                    product(acc2[:, v, :], group * u + v, zq[:], zs[:])
+                res = keep.tile([P, group, CHUNK], F32, name=f"o{c}{u}", align_bytes=64)
+                if c < 2 or (c == 3 and u == 0):
+                    nc.scalar.activation(res[:], acc2[:], COPY, scale=0.0625)
+                else:
+                    nc.vector.tensor_scalar(res[:], acc2[:], 0.0625, None, MULT)
+                nc.sync.dma_start(
+                    out=out_v[:, group * u : group * (u + 1), c * CHUNK : (c + 1) * CHUNK], in_=res[:]
+                )

@@ -36,7 +36,7 @@ def tile_picked_pqtwice_tanh_p_kernel(
         dsc_win = keep.tile([P, TABLE], U8, name="dsc_win", align_bytes=64)
         xsc_win = keep.tile([P, TABLE], U8, name="xsc_win", align_bytes=64)
         dw_win = keep.tile([P, TABLE], U32, name="dw_win", align_bytes=64)
-        xw_win = keep.tile([P, TABLE], U32, name="xw_win", align_bytes=64)
+        xw_win = keep.tile([P, TABLE], U32, name="xw_win", tag="xw_win", align_bytes=64)
         gs_t = keep.tile([P, PACK], F32, name="gs_t")
         warm = keep.tile([P, 2], F32, name="warm")
 
@@ -68,29 +68,28 @@ def tile_picked_pqtwice_tanh_p_kernel(
             nc.sync.dma_start(out=dsc[j:P:32, :].bitcast(I32), in_=dsc[8 * j : P : 32, :].bitcast(I32))
 
         dw_g = keep.tile([P, S], U32, name="dw_g", align_bytes=64)
-        dw = keep.tile([P, S], U32, name="dw", align_bytes=64)
-        dealt = dw[:].rearrange("p (t m) -> p m t", t=PACK)
         picked = dw_g[:].rearrange("p (m t) -> p m t", t=PACK)
         nc.vector.tensor_copy(dw_g[:], dw_win[:].indirect(k1_t[:]))
         xsc = keep.tile([P, S], U8, name="xsc", align_bytes=64)
         nc.vector.tensor_copy(xsc[:], xsc_win[:].indirect(offs_t[:]))
-        nc.vector.tensor_copy(dealt[:, :, 0:1], picked[:, :, 0:1])
+        dw_lo = keep.tile([P, HALF], U32, name="dw_lo", align_bytes=64)
+        nc.vector.tensor_copy(dw_lo[:].rearrange("p (t m) -> p m t", t=2), picked[:, :, 0:2])
 
         xw = keep.tile([P, S], U32, name="xw", align_bytes=64)
         for c in range(2):
             nc.vector.tensor_copy(xw[:, c * HALF : (c + 1) * HALF], xw_win[:].indirect(offs_t[:, 16 * c : 16 * (c + 1)]))
-        nc.vector.tensor_copy(dealt[:, :, 1:PACK], picked[:, :, 1:PACK])
+        dw_hi = keep.tile([P, HALF], U32, name="dw_hi", tag="xw_win", align_bytes=64)
+        nc.vector.tensor_copy(dw_hi[:].rearrange("p (t m) -> p m t", t=2), picked[:, :, 2:4])
+        dw = [dw_lo[:, 0:P], dw_lo[:, P:HALF], dw_hi[:, 0:P], dw_hi[:, P:HALF]]
 
-        zg = keep.tile([P, PACK * S + CHUNK], BF16, name="zg", align_bytes=64)
-        h = [keep.tile([P, S], F32, name=f"h{t}", align_bytes=64)[:] for t in range(PACK - 1)]
-        h.append(zg[:, 2 * S + CHUNK :].bitcast(F32))
+        h = [keep.tile([P, S], F32, name=f"h{t}", align_bytes=64) for t in range(PACK)]
         hz = [keep.tile([P, S], F32, name=f"hz{t}", align_bytes=64) for t in range(PACK)]
 
         def product(acc, t, words, scales):
             cols = slice(P * t, P * (t + 1))
             nc.tensor.matmul_mx(
                 out=acc,
-                lhsT=dw[:, cols].bitcast(FP8X4),
+                lhsT=dw[t].bitcast(FP8X4),
                 lhsT_scale=dsc[:, cols],
                 rhs=words.bitcast(FP8X4),
                 rhs_scale=scales,
@@ -103,56 +102,72 @@ def tile_picked_pqtwice_tanh_p_kernel(
             product(acc[:], t, xw[:, part], xsc[:, part])
             nc.scalar.activation(h[t][:, part], acc[:], TANH, scale=0.0625)
 
-        def weigh(t):
-            nc.scalar.activation(hz[t][:], h[t], COPY, scale=gs_t[:, t : t + 1])
-
-        def fetch(t, c0, width):
-            lst = nb_t[:, c0 // 16 : (c0 + width) // 16]
-            nc.vector.tensor_copy(zg[:, S * t + c0 : S * t + c0 + width], hz[t][:].indirect(lst))
+        def weigh(t, part):
+            nc.scalar.activation(hz[t][:, part], h[t][:, part], COPY, scale=gs_t[:, t : t + 1])
 
         for c in range(2):
             part = slice(c * HALF, (c + 1) * HALF)
-            first(0, part, c)
-            nc.vector.tensor_scalar(hz[0][:, part], h[0][:, part], gs_t[:, 0:1], None, MULT)
-        whole = slice(0, S)
-        first(1, whole, 2)
-        first(2, whole, 3)
-        weigh(1)
-        first(3, whole, 4)
-        weigh(2)
-        weigh(3)
-
-        for t in range(2):
-            for c0 in range(0, S, HALF):
-                fetch(t, c0, HALF)
+            for t in range(2):
+                first(t, part, 2 * c + t)
+                nc.vector.tensor_scalar(hz[t][:, part], h[t][:, part], gs_t[:, t : t + 1], None, MULT)
+        first(2, slice(0, S), 4)
+        first(3, slice(0, S), 5)
+        weigh(2, slice(0, S - 64))
+        weigh(3, slice(0, S))
+        weigh(2, slice(S - 64, S))
 
         chunks = S // CHUNK
-        planes = zg[:, 0 : PACK * S].rearrange("p (t n) -> p t n", t=PACK)
-        zi = [keep.tile([P, CHUNK, PACK], BF16, name=f"zi{c}", align_bytes=64) for c in range(chunks)]
-        for c in range(chunks):
-            fetch(2, c * CHUNK, CHUNK)
-            fetch(3, c * CHUNK, CHUNK)
-            dst = zi[c][:].rearrange("p (n i) t -> p n t i", i=4)
+        span = PACK * CHUNK
+        pitch = S - CHUNK + span
+        work = keep.tile([P, PACK * pitch], BF16, name="work", align_bytes=64)
+        planes = work[:].rearrange("p (t n) -> p t n", t=PACK)
+        spare = [keep.tile([P, span], BF16, name="spare", align_bytes=64)[:]] * 2
+        zi = [planes[:, 2, S - CHUNK :], planes[:, 3, S - CHUNK :]] + spare
+        zq = [keep.tile([P, CHUNK], U32, name=f"zq{c}", align_bytes=64) for c in range(chunks)]
+        zs = [keep.tile([P, CHUNK], U8, name=f"zs{c}", align_bytes=64) for c in range(chunks)]
+
+        def fetch(t, c0, width):
+            lst = nb_t[:, c0 // 16 : (c0 + width) // 16]
+            nc.vector.tensor_copy(planes[:, t, c0 : c0 + width], hz[t][:].indirect(lst))
+
+        def weave(c):
+            dst = zi[c].rearrange("p (n i t) -> p n t i", i=4, t=PACK)
             src = planes[:, :, c * CHUNK : (c + 1) * CHUNK].rearrange("p t (n i) -> p n t i", i=4)
             if c < chunks - 1:
                 nc.scalar.copy(dst, src)
             else:
                 nc.vector.tensor_copy(dst, src)
 
+        def quantise(c):
+            nc.vector.quantize_mx(out=zq[c][:].bitcast(FP8X4), scales=zs[c][:], in_=zi[c])
+
+        for t in range(2):
+            for c0 in range(0, S, HALF):
+                fetch(t, c0, HALF)
+        for c in range(chunks - 1):
+            fetch(2, c * CHUNK, CHUNK)
+            fetch(3, c * CHUNK, CHUNK)
+            weave(c)
+        last = S - CHUNK
+        quantise(0)
+        fetch(2, last, CHUNK)
+        quantise(1)
+        fetch(3, last, CHUNK)
+        quantise(2)
+        weave(3)
+        quantise(3)
+
         out_v = out.rearrange("(p t) n -> p t n", t=PACK)
-        bank = 5
+        bank = 6
         for c in range(chunks):
-            zq = keep.tile([P, CHUNK], U32, name=f"zq{c}", align_bytes=64)
-            zs = keep.tile([P, CHUNK], U8, name=f"zs{c}", align_bytes=64)
-            nc.vector.quantize_mx(out=zq[:].bitcast(FP8X4), scales=zs[:], in_=zi[c][:].rearrange("p n t -> p (n t)"))
             group = PACK if c < chunks - 1 else 2
             for u in range(PACK // group):
                 acc2 = psum.tile([P, group, CHUNK], F32, name="acc2", tag=f"bank{bank % 8}")
                 bank += 1
                 for v in range(group):
-                    product(acc2[:, v, :], group * u + v, zq[:], zs[:])
+                    product(acc2[:, v, :], group * u + v, zq[c][:], zs[c][:])
                 res = keep.tile([P, group, CHUNK], F32, name=f"o{c}{u}", align_bytes=64)
-                if c < 2 or (c == 3 and u == 0):
+                if u == 0:
                     nc.scalar.activation(res[:], acc2[:], COPY, scale=0.0625)
                 else:
                     nc.vector.tensor_scalar(res[:], acc2[:], 0.0625, None, MULT)

@@ -28,6 +28,7 @@ def tile_picked_pqtwice_tanh_p_kernel(
     nc = tc.nc
     with ExitStack() as ctx:
         keep = ctx.enter_context(tc.tile_pool(name="keep", bufs=1))
+        shared = ctx.enter_context(tc.tile_pool(name="shared", bufs=1))
         psum = ctx.enter_context(tc.psum_pool(name="psum", bufs=1))
 
         k1_t = keep.tile([P, S // 16], U16, name="k1_t")
@@ -36,12 +37,10 @@ def tile_picked_pqtwice_tanh_p_kernel(
         dsc_win = keep.tile([P, TABLE], U8, name="dsc_win", align_bytes=64)
         xsc_win = keep.tile([P, TABLE], U8, name="xsc_win", align_bytes=64)
         dw_win = keep.tile([P, TABLE], U32, name="dw_win", align_bytes=64)
-        xw_win = keep.tile([P, TABLE], U32, name="xw_win", tag="xw_win", align_bytes=64)
+        xw_win = shared.tile([P, TABLE], U32, name="xw_win", align_bytes=64, offset=0)
         gs_t = keep.tile([P, PACK], F32, name="gs_t")
-        warm = keep.tile([P, 2], F32, name="warm")
 
         nc.vector.memset(xsc_win[:].bitcast(I32), 0)
-        nc.vector.memset(warm[:, 0:1], 0.0)
         nc.sync.dma_start(k1_t[:], k1)
         nc.sync.dma_start(
             out=dsc_win[:].bitcast(I32),
@@ -49,20 +48,19 @@ def tile_picked_pqtwice_tanh_p_kernel(
         )
         nc.sync.dma_start(out=dw_win[:].bitcast(I32), in_=d_words[0].rearrange("p n t -> p (n t)").bitcast(I32))
         nc.sync.dma_start(offs_t[:], offs)
-        nc.sync.dma_start(nb_t[:], nb)
         for q in range(4):
             nc.scalar.dma_start(
                 out=xsc_win[32 * q : 32 * q + 4, :].bitcast(I32), in_=x_scales[0, 4 * q : 4 * q + 4, :].bitcast(I32)
             )
+        nc.sync.dma_start(nb_t[:], nb)
         nc.sync.dma_start(out=xw_win[:].bitcast(I32), in_=x_words[0].rearrange("p n t -> p (n t)").bitcast(I32))
-        nc.gpsimd.dma_start(out=gs_t[:], in_=gs.rearrange("(p t) o -> p (t o)", t=PACK))
-        nc.scalar.activation(warm[:, 1:2], warm[:, 0:1], TANH)
+        nc.sync.dma_start(out=gs_t[:], in_=gs.rearrange("(p t) o -> p (t o)", t=PACK))
 
         dsc_g = keep.tile([P, S], U8, name="dsc_g", align_bytes=64)
         dsc = keep.tile([P, S], U8, name="dsc", align_bytes=64)
         nc.vector.tensor_copy(dsc_g[:], dsc_win[:].indirect(k1_t[:]))
         nc.vector.tensor_copy(
-            dsc[:].rearrange("p (t m) -> p m t", t=PACK), dsc_g[:].rearrange("p (m t) -> p m t", t=PACK)
+            dsc[:].rearrange("p (t m) -> p t m", t=PACK), dsc_g[:].rearrange("p (m t) -> p t m", t=PACK)
         )
         for j in range(1, 4):
             nc.sync.dma_start(out=dsc[j:P:32, :].bitcast(I32), in_=dsc[8 * j : P : 32, :].bitcast(I32))
@@ -70,17 +68,32 @@ def tile_picked_pqtwice_tanh_p_kernel(
         dw_g = keep.tile([P, S], U32, name="dw_g", align_bytes=64)
         picked = dw_g[:].rearrange("p (m t) -> p m t", t=PACK)
         nc.vector.tensor_copy(dw_g[:], dw_win[:].indirect(k1_t[:]))
+        for b in (6, 7):
+            idle = psum.tile([P, S], F32, name="idle", tag=f"bank{b}")
+            nc.tensor.matmul_mx(
+                out=idle[:],
+                lhsT=dw_g[:, 0:P].bitcast(FP8X4),
+                lhsT_scale=dsc_g[:, 0:P],
+                rhs=dw_g[:].bitcast(FP8X4),
+                rhs_scale=dsc_g[:],
+                start=True,
+                stop=True,
+            )
         xsc = keep.tile([P, S], U8, name="xsc", align_bytes=64)
         nc.vector.tensor_copy(xsc[:], xsc_win[:].indirect(offs_t[:]))
-        dw_lo = keep.tile([P, HALF], U32, name="dw_lo", align_bytes=64)
-        nc.vector.tensor_copy(dw_lo[:].rearrange("p (t m) -> p m t", t=2), picked[:, :, 0:2])
+
+        def deal(words, t0, t1):
+            nc.vector.tensor_copy(words[:].rearrange("p (t m) -> p m t", m=P), picked[:, :, t0:t1])
+
+        dw01 = keep.tile([P, HALF], U32, name="dw01", align_bytes=64)
+        deal(dw01, 0, 2)
 
         xw = keep.tile([P, S], U32, name="xw", align_bytes=64)
         for c in range(2):
             nc.vector.tensor_copy(xw[:, c * HALF : (c + 1) * HALF], xw_win[:].indirect(offs_t[:, 16 * c : 16 * (c + 1)]))
-        dw_hi = keep.tile([P, HALF], U32, name="dw_hi", tag="xw_win", align_bytes=64)
-        nc.vector.tensor_copy(dw_hi[:].rearrange("p (t m) -> p m t", t=2), picked[:, :, 2:4])
-        dw = [dw_lo[:, 0:P], dw_lo[:, P:HALF], dw_hi[:, 0:P], dw_hi[:, P:HALF]]
+        dw23 = shared.tile([P, HALF], U32, name="dw23", align_bytes=64, offset=0)
+        deal(dw23, 2, 4)
+        dw = [dw01[:, 0:P], dw01[:, P:HALF], dw23[:, 0:P], dw23[:, P:HALF]]
 
         h = [keep.tile([P, S], F32, name=f"h{t}", align_bytes=64) for t in range(PACK)]
         hz = [keep.tile([P, S], F32, name=f"hz{t}", align_bytes=64) for t in range(PACK)]
@@ -109,8 +122,10 @@ def tile_picked_pqtwice_tanh_p_kernel(
             part = slice(c * HALF, (c + 1) * HALF)
             for t in range(2):
                 first(t, part, 2 * c + t)
-                nc.vector.tensor_scalar(hz[t][:, part], h[t][:, part], gs_t[:, t : t + 1], None, MULT)
+                if (c, t) != (1, 1):
+                    nc.vector.tensor_scalar(hz[t][:, part], h[t][:, part], gs_t[:, t : t + 1], None, MULT)
         first(2, slice(0, S), 4)
+        weigh(1, slice(HALF, S))
         first(3, slice(0, S), 5)
         weigh(2, slice(0, S - 64))
         weigh(3, slice(0, S))
@@ -160,17 +175,18 @@ def tile_picked_pqtwice_tanh_p_kernel(
         out_v = out.rearrange("(p t) n -> p t n", t=PACK)
         bank = 6
         for c in range(chunks):
-            group = PACK if c < chunks - 1 else 2
+            group = 2 if c < chunks - 1 else 1
             for u in range(PACK // group):
                 acc2 = psum.tile([P, group, CHUNK], F32, name="acc2", tag=f"bank{bank % 8}")
                 bank += 1
                 for v in range(group):
                     product(acc2[:, v, :], group * u + v, zq[c][:], zs[c][:])
                 res = keep.tile([P, group, CHUNK], F32, name=f"o{c}{u}", align_bytes=64)
-                if u == 0:
+                if group == 2 or u % 2 == 0:
                     nc.scalar.activation(res[:], acc2[:], COPY, scale=0.0625)
                 else:
                     nc.vector.tensor_scalar(res[:], acc2[:], 0.0625, None, MULT)
-                nc.sync.dma_start(
+                queue = nc.scalar if group == 1 and u % 2 == 0 else nc.sync
+                queue.dma_start(
                     out=out_v[:, group * u : group * (u + 1), c * CHUNK : (c + 1) * CHUNK], in_=res[:]
                 )

from contextlib import ExitStack

import concourse.mybir as mybir

F32 = mybir.dt.float32
BF16 = mybir.dt.bfloat16
I32 = mybir.dt.int32
U32 = mybir.dt.uint32
U16 = mybir.dt.uint16
U8 = mybir.dt.uint8
FP8X4 = mybir.dt.float8_e4m3fn_x4
TANH = mybir.ActivationFunctionType.Tanh
COPY = mybir.ActivationFunctionType.Copy
MULT = mybir.AluOpType.mult

P = 128
PACK = 4
S = 512
TABLE = 2048
HALF = 256
CHUNK = 128
FLOPS = 2 * 2 * 512 * 512 * 512


def tile_picked_pqtwice_tanh_p_kernel(
    tc, x_words, x_scales, d_words, d_scales, gs, offs, k1, nb, out
):
    nc = tc.nc
    with ExitStack() as ctx:
        keep = ctx.enter_context(tc.tile_pool(name="keep", bufs=1))
        shared = ctx.enter_context(tc.tile_pool(name="shared", bufs=1))
        psum = ctx.enter_context(tc.psum_pool(name="psum", bufs=1))

        k1_t = keep.tile([P, S // 16], U16, name="k1_t")
        offs_t = keep.tile([P, S // 16], U16, name="offs_t")
        nb_t = keep.tile([P, S // 16], U16, name="nb_t")
        dsc_win = keep.tile([P, TABLE], U8, name="dsc_win", align_bytes=64)
        xsc_win = keep.tile([P, TABLE], U8, name="xsc_win", align_bytes=64)
        dw_win = keep.tile([P, TABLE], U32, name="dw_win", align_bytes=64)
        xw_win = shared.tile([P, TABLE], U32, name="xw_win", align_bytes=64, offset=0)
        gs_t = keep.tile([P, PACK], F32, name="gs_t")

        nc.vector.memset(xsc_win[:].bitcast(I32), 0)
        nc.sync.dma_start(k1_t[:], k1)
        nc.sync.dma_start(
            out=dsc_win[:].bitcast(I32),
            in_=d_scales.rearrange("z q c -> q z c").bitcast(I32).to_broadcast([16, 8, TABLE // 4]),
        )
        nc.sync.dma_start(out=dw_win[:].bitcast(I32), in_=d_words[0].rearrange("p n t -> p (n t)").bitcast(I32))
        nc.sync.dma_start(offs_t[:], offs)
        for q in range(4):
            nc.scalar.dma_start(
                out=xsc_win[32 * q : 32 * q + 4, :].bitcast(I32), in_=x_scales[0, 4 * q : 4 * q + 4, :].bitcast(I32)
            )
        nc.sync.dma_start(nb_t[:], nb)
        nc.sync.dma_start(out=xw_win[:].bitcast(I32), in_=x_words[0].rearrange("p n t -> p (n t)").bitcast(I32))
        nc.sync.dma_start(out=gs_t[:], in_=gs.rearrange("(p t) o -> p (t o)", t=PACK))

        dsc_g = keep.tile([P, S], U8, name="dsc_g", align_bytes=64)
        dsc = keep.tile([P, S], U8, name="dsc", align_bytes=64)
        nc.vector.tensor_copy(dsc_g[:], dsc_win[:].indirect(k1_t[:]))
        nc.vector.tensor_copy(
            dsc[:].rearrange("p (t m) -> p t m", t=PACK), dsc_g[:].rearrange("p (m t) -> p t m", t=PACK)
        )
        for j in range(1, 4):
            nc.sync.dma_start(out=dsc[j:P:32, :].bitcast(I32), in_=dsc[8 * j : P : 32, :].bitcast(I32))

        dw_g = keep.tile([P, S], U32, name="dw_g", align_bytes=64)
        picked = dw_g[:].rearrange("p (m t) -> p m t", t=PACK)
        nc.vector.tensor_copy(dw_g[:], dw_win[:].indirect(k1_t[:]))
        for b in (6, 7):
            idle = psum.tile([P, S], F32, name="idle", tag=f"bank{b}")
            nc.tensor.matmul_mx(
                out=idle[:],
                lhsT=dw_g[:, 0:P].bitcast(FP8X4),
                lhsT_scale=dsc_g[:, 0:P],
                rhs=dw_g[:].bitcast(FP8X4),
                rhs_scale=dsc_g[:],
                start=True,
                stop=True,
            )
        xsc = keep.tile([P, S], U8, name="xsc", align_bytes=64)
        nc.vector.tensor_copy(xsc[:], xsc_win[:].indirect(offs_t[:]))

        def deal(words, t0, t1):
            nc.vector.tensor_copy(words[:].rearrange("p (t m) -> p m t", m=P), picked[:, :, t0:t1])

        dw01 = keep.tile([P, HALF], U32, name="dw01", align_bytes=64)
        deal(dw01, 0, 2)

        xw = keep.tile([P, S], U32, name="xw", align_bytes=64)
        for c in range(2):
            nc.vector.tensor_copy(xw[:, c * HALF : (c + 1) * HALF], xw_win[:].indirect(offs_t[:, 16 * c : 16 * (c + 1)]))
        dw23 = shared.tile([P, HALF], U32, name="dw23", align_bytes=64, offset=0)
        deal(dw23, 2, 4)
        dw = [dw01[:, 0:P], dw01[:, P:HALF], dw23[:, 0:P], dw23[:, P:HALF]]

        h = [keep.tile([P, S], F32, name=f"h{t}", align_bytes=64) for t in range(PACK)]
        hz = [keep.tile([P, S], F32, name=f"hz{t}", align_bytes=64) for t in range(PACK)]

        def product(acc, t, words, scales):
            cols = slice(P * t, P * (t + 1))
            nc.tensor.matmul_mx(
                out=acc,
                lhsT=dw[t].bitcast(FP8X4),
                lhsT_scale=dsc[:, cols],
                rhs=words.bitcast(FP8X4),
                rhs_scale=scales,
                start=True,
                stop=True,
            )

        def first(t, part, bank):
            acc = psum.tile([P, part.stop - part.start], F32, name="acc", tag=f"bank{bank}")
            product(acc[:], t, xw[:, part], xsc[:, part])
            nc.scalar.activation(h[t][:, part], acc[:], TANH, scale=0.0625)

        def weigh(t, part):
            nc.scalar.activation(hz[t][:, part], h[t][:, part], COPY, scale=gs_t[:, t : t + 1])

        for c in range(2):
            part = slice(c * HALF, (c + 1) * HALF)
            for t in range(2):
                first(t, part, 2 * c + t)
                if (c, t) != (1, 1):
                    nc.vector.tensor_scalar(hz[t][:, part], h[t][:, part], gs_t[:, t : t + 1], None, MULT)
        first(2, slice(0, S), 4)
        weigh(1, slice(HALF, S))
        first(3, slice(0, S), 5)
        weigh(2, slice(0, S - 64))
        weigh(3, slice(0, S))
        weigh(2, slice(S - 64, S))

        chunks = S // CHUNK
        span = PACK * CHUNK
        pitch = S - CHUNK + span
        work = keep.tile([P, PACK * pitch], BF16, name="work", align_bytes=64)
        planes = work[:].rearrange("p (t n) -> p t n", t=PACK)
        spare = [keep.tile([P, span], BF16, name="spare", align_bytes=64)[:]] * 2
        zi = [planes[:, 2, S - CHUNK :], planes[:, 3, S - CHUNK :]] + spare
        zq = [keep.tile([P, CHUNK], U32, name=f"zq{c}", align_bytes=64) for c in range(chunks)]
        zs = [keep.tile([P, CHUNK], U8, name=f"zs{c}", align_bytes=64) for c in range(chunks)]

        def fetch(t, c0, width):
            lst = nb_t[:, c0 // 16 : (c0 + width) // 16]
            nc.vector.tensor_copy(planes[:, t, c0 : c0 + width], hz[t][:].indirect(lst))

        def weave(c):
            dst = zi[c].rearrange("p (n i t) -> p n t i", i=4, t=PACK)
            src = planes[:, :, c * CHUNK : (c + 1) * CHUNK].rearrange("p t (n i) -> p n t i", i=4)
            if c < chunks - 1:
                nc.scalar.copy(dst, src)
            else:
                nc.vector.tensor_copy(dst, src)

        def quantise(c):
            nc.vector.quantize_mx(out=zq[c][:].bitcast(FP8X4), scales=zs[c][:], in_=zi[c])

        for t in range(2):
            for c0 in range(0, S, HALF):
                fetch(t, c0, HALF)
        for c in range(chunks - 1):
            fetch(2, c * CHUNK, CHUNK)
            fetch(3, c * CHUNK, CHUNK)
            weave(c)
        last = S - CHUNK
        quantise(0)
        fetch(2, last, CHUNK)
        quantise(1)
        fetch(3, last, CHUNK)
        quantise(2)
        weave(3)
        quantise(3)

        out_v = out.rearrange("(p t) n -> p t n", t=PACK)
        bank = 6
        for c in range(chunks):
            group = 2 if c < chunks - 1 else 1
            for u in range(PACK // group):
                acc2 = psum.tile([P, group, CHUNK], F32, name="acc2", tag=f"bank{bank % 8}")
                bank += 1
                for v in range(group):
                    product(acc2[:, v, :], group * u + v, zq[c][:], zs[c][:])
                res = keep.tile([P, group, CHUNK], F32, name=f"o{c}{u}", align_bytes=64)
                if group == 2 or u % 2 == 0:
                    nc.scalar.activation(res[:], acc2[:], COPY, scale=0.0625)
                else:
                    nc.vector.tensor_scalar(res[:], acc2[:], 0.0625, None, MULT)
                queue = nc.scalar if group == 1 and u % 2 == 0 else nc.sync
                queue.dma_start(
                    out=out_v[:, group * u : group * (u + 1), c * CHUNK : (c + 1) * CHUNK], in_=res[:]
                )
